import numpy as np
import ml_dtypes


def mxq(x, axis, fmt="e4m3"):
    dtype, down = {"e4m3": (ml_dtypes.float8_e4m3fn, 7), "e5m2": (ml_dtypes.float8_e5m2, 14)}[fmt]
    v = np.moveaxis(np.asarray(x, np.float32).astype(ml_dtypes.bfloat16).astype(np.float64), axis, -1)
    blocks = v.reshape(v.shape[:-1] + (-1, 32))
    amax = np.abs(blocks).max(-1, keepdims=True)
    byte = np.maximum(np.where(amax > 0, np.frexp(amax)[1] - 1 + 127, 0) - down, 1)
    scale = np.exp2(byte - 127.0)
    codes = (blocks / scale).astype(np.float32).astype(dtype).astype(np.float64)
    return np.moveaxis((codes * scale).reshape(v.shape), -1, axis)


WIDE = False


def mx_kscale(k):
    if not WIDE:
        return np.ones(k)
    levels = np.array([10, -10, 5, -5, 0])
    if k % 512:
        return np.exp2(np.random.permutation(np.resize(levels, k // 32))).repeat(32)
    a = np.empty((k // 512, 16))
    for p in range(k // 512):
        a[p, :8] = np.random.permutation(np.resize(levels, 8))
        for g in range(8):
            far = levels[np.abs(levels - a[p, g]) >= 10]
            a[p, g + 8] = far[np.random.randint(len(far))]
    return np.exp2(a.ravel()).repeat(32)


def f64(x):
    return np.asarray(x).astype(np.float64)


def striped(idx):
    return np.tile(idx.reshape(-1, 16).T, (8, 1)).astype(np.uint16)


def unstriped(offs):
    return offs[:16].T.reshape(-1).astype(np.int64)


def striped8(idx):
    return np.concatenate([x.reshape(-1, 16).T for x in idx]).astype(np.uint16)


def runs(offs, k):
    lists = np.stack([offs[16 * r : 16 * r + 16].T.reshape(-1) for r in range(8)]).astype(np.int64)
    return lists[np.arange(k) % 512 // 64]


def pack_weight(w):
    k, n = w.shape
    w = f64(np.asarray(w, np.float32).astype(ml_dtypes.bfloat16)).reshape(k // 32, 32, n)
    amax = np.abs(w).max(1)
    byte = np.clip(np.where(amax > 0, np.frexp(amax)[1] - 1 + 127 - 7, 1), 1, 254)
    scaled = (w * np.exp2(127.0 - byte)[:, None, :]).reshape(k, n).astype(np.float32)
    words = np.ascontiguousarray(scaled.reshape(k // 512, 128, 4, n).transpose(0, 1, 3, 2)).astype(ml_dtypes.float8_e4m3fn).view(np.uint8)
    return words, np.ascontiguousarray(byte.astype(np.uint8).reshape(k // 512, 16, n))


def unpack_weight(words, scales):
    g, p, n, _ = words.shape
    vals = np.ascontiguousarray(words).view(ml_dtypes.float8_e4m3fn).astype(np.float64) * np.repeat(np.exp2(scales.astype(np.float64) - 127.0), 8, axis=1)[..., None]
    return vals.transpose(0, 1, 3, 2).reshape(g * 512, n)


K, T, S, H, G = 512, 2048, 512, 512, 2048


def setup_inputs():
    n = np.random.standard_normal
    s = mx_kscale(K)[:, None]
    packed_xT = pack_weight(n((K, T)) * s)
    packed_dT = pack_weight(n((K, G)) / s)
    return {
        "x_words": packed_xT[0],
        "x_scales": packed_xT[1],
        "w1": (n((K, H)) / np.sqrt(K) / s).astype(np.float32),
        "gs": (np.random.uniform(0.5, 1.5, (K, 1)) * s).astype(np.float32),
        "d_words": packed_dT[0],
        "d_scales": packed_dT[1],
        "offs": striped(np.random.permutation(T)[:S]),
        "c1": striped8(np.stack([np.random.permutation(S) for _ in range(8)])),
        "c2": striped8(np.stack([np.random.permutation(S) for _ in range(8)])),
        "kq": striped8(np.random.randint(0, G, (8, H))),
    }


def reference(x_words, x_scales, w1, gs, d_words, d_scales, offs, c1, c2, kq):
    d_kq = unpack_weight(d_words, d_scales)[np.arange(K)[:, None], runs(kq, K)]
    xq = unpack_weight(x_words, x_scales)[:, unstriped(offs)]
    y = mxq(f64(w1), 0, "e4m3").T @ xq
    a = y[np.arange(H)[:, None], runs(c1, H)]
    b = y[np.arange(H)[:, None], runs(c2, H)]
    z = f64(gs) * ((a * b) / (np.maximum(np.abs(a), np.abs(b)) + 0.05))
    return 0.0625 * ((d_kq.T @ mxq(z, 0, "e4m3")))

@@ -1,0 +1,178 @@
+from contextlib import ExitStack
+
+import concourse.mybir as mybir
+
+K, T, S, H, G = 512, 2048, 512, 512, 2048
+FLOPS = 2 * K * H * S * 2
+
+F32 = mybir.dt.float32
+BF16 = mybir.dt.bfloat16
+I32 = mybir.dt.int32
+U32 = mybir.dt.uint32
+U16 = mybir.dt.uint16
+U8 = mybir.dt.uint8
+FP8X4 = mybir.dt.float8_e4m3fn_x4
+ALU = mybir.AluOpType
+ACT = mybir.ActivationFunctionType
+
+P = 128
+PACK = 4
+CHUNKS = (256, 128, 128)
+M_VEC = 40
+
+
+def tile_picked_minsum2_none_p_kernel(
+    tc, x_words, x_scales, w1, gs, d_words, d_scales, offs, c1, c2, kq, out
+):
+    nc = tc.nc
+    with ExitStack() as ctx:
+        keep = ctx.enter_context(tc.tile_pool(name="keep", bufs=1))
+        psum = ctx.enter_context(tc.psum_pool(name="psum", bufs=1))
+
+        def load_list(name, src):
+            t = keep.tile([P, S // 16], U16, name=name)
+            nc.sync.dma_start(t[:], src)
+            return t
+
+        xs_table = keep.tile([P, T], U8, name="xs_table")
+        ds_table = keep.tile([P, G], U8, name="ds_table")
+        d_plane = keep.tile([P, H], U8, name="d_plane", align_bytes=64)
+        seed = keep.tile([P, 1], F32, name="seed")
+        shift = keep.tile([P, 1], F32, name="shift")
+        nc.vector.memset(xs_table[:].bitcast(I32), 0)
+        nc.vector.memset(seed[:], 400.0)
+        nc.scalar.activation(shift[:], seed[:], ACT.Abs_reciprocal_sqrt)
+        nc.vector.memset(ds_table[:].bitcast(I32), 0)
+        nc.vector.memset(d_plane[:].bitcast(I32), 0)
+
+        offs_sb = load_list("offs_sb", offs)
+        xw_table = keep.tile([P, T], U32, name="xw_table")
+        nc.sync.dma_start(xw_table[:].bitcast(I32), x_words[0].rearrange("p n t -> p (n t)").bitcast(I32))
+        xs_rows = x_scales[0].bitcast(I32)
+        for q in range(4):
+            nc.sync.dma_start(xs_table[:].bitcast(I32)[32 * q : 32 * q + 4, :], xs_rows[4 * q : 4 * q + 4, :])
+        w_rows = w1.rearrange("(p j) c -> p j c", j=PACK)
+        w_raw = []
+        for h in range(2):
+            t = keep.tile([P, PACK, H // 2], F32, name=f"w_raw{h}")
+            nc.sync.dma_start(t[:], w_rows[:, :, h * (H // 2) : (h + 1) * (H // 2)])
+            w_raw.append(t)
+        kq_sb = load_list("kq_sb", kq)
+        ds_rows = d_scales[0].bitcast(I32)
+        for e in range(2):
+            nc.sync.dma_start(ds_table[:].bitcast(I32)[e:P:16, :], ds_rows[e:16:2, :])
+        c1_sb = load_list("c1_sb", c1)
+        c2_sb = load_list("c2_sb", c2)
+        gs_sb = keep.tile([P, PACK], F32, name="gs_sb")
+        nc.sync.dma_start(gs_sb[:], gs.rearrange("(p t) o -> p (t o)", t=PACK))
+        dw_table = keep.tile([P, G], U32, name="dw_table")
+        nc.sync.dma_start(dw_table[:].bitcast(I32), d_words[0].rearrange("p n t -> p (n t)").bitcast(I32))
+
+        x_codes = keep.tile([P, S], U32, name="x_codes", align_bytes=64)
+        x_plane = keep.tile([P, S], U8, name="x_plane", align_bytes=64)
+        nc.vector.tensor_copy(x_codes[:], xw_table[:].indirect(offs_sb[:]))
+        nc.vector.tensor_copy(x_plane[:], xs_table[:].indirect(offs_sb[:]))
+
+        w_bf = keep.tile([P, PACK, P, PACK], BF16, name="w_bf", align_bytes=64)
+
+        def deal(copy, h, m0, m1):
+            src = w_raw[h][:, :, PACK * m0 : PACK * m1].rearrange("p j (m t) -> p m j t", t=PACK)
+            dst = w_bf[:, :, 64 * h + m0 : 64 * h + m1, :].rearrange("p t m j -> p m j t")
+            copy(dst, src)
+
+        deal(nc.scalar.copy, 0, 0, 64)
+        deal(nc.vector.tensor_copy, 1, 0, M_VEC)
+        deal(nc.scalar.copy, 1, M_VEC, 64)
+
+        y = []
+        for t in range(PACK):
+            w_codes = keep.tile([P, P], U32, name=f"w_codes{t}", align_bytes=64)
+            w_plane = keep.tile([P, P], U8, name=f"w_plane{t}", align_bytes=64)
+            nc.vector.quantize_mx(
+                out=w_codes[:].bitcast(FP8X4), scales=w_plane[:], in_=w_bf[:, t].rearrange("p m j -> p (m j)")
+            )
+            y_ps = psum.tile([P, S], F32, name=f"y_ps{t}")
+            nc.tensor.matmul_mx(
+                out=y_ps[:], lhsT=w_codes[:].bitcast(FP8X4), lhsT_scale=w_plane[:],
+                rhs=x_codes[:].bitcast(FP8X4), rhs_scale=x_plane[:], start=True, stop=True,
+            )
+            y_t = keep.tile([P, S], F32, name=f"y{t}")
+            nc.scalar.copy(y_t[:], y_ps[:])
+            y.append(y_t)
+
+        ds_picked = keep.tile([P, H], U8, name="ds_picked")
+        nc.vector.tensor_copy(ds_picked[:], ds_table[:].indirect(kq_sb[:]))
+        for i in range(4):
+            first = 16 * (i // 2) + i % 2
+            nc.sync.dma_start(d_plane[:].bitcast(I32)[i:P:32, :], ds_picked[:].bitcast(I32)[first:P:32, :])
+        d_codes = keep.tile([P, H], U32, name="d_codes", align_bytes=64)
+
+        starts = [sum(CHUNKS[:c]) for c in range(len(CHUNKS))]
+        st = {}
+
+        def gather(c):
+            n, j0 = CHUNKS[c], starts[c]
+            ab = keep.tile([P, PACK, 2, n], F32, name=f"ab{c}")
+            mag = keep.tile([P, PACK, 2, n], F32, name=f"mag{c}")
+            for t in range(PACK):
+                for s, lst in enumerate((c1_sb, c2_sb)):
+                    nc.vector.tensor_copy(ab[:, t, s, :], y[t][:].indirect(lst[:, j0 // 16 : (j0 + n) // 16]))
+                nc.scalar.activation(mag[:, t], ab[:, t], ACT.Abs)
+            st[c] = (ab, mag)
+
+        def larger(c):
+            n = CHUNKS[c]
+            ab, mag = st[c]
+            big = keep.tile([P, PACK, n], F32, name=f"big{c}")
+            root = keep.tile([P, PACK, n], F32, name=f"root{c}")
+            inv = keep.tile([P, PACK, n], F32, name=f"inv{c}")
+            for u in range(2):
+                pl = slice(2 * u, 2 * u + 2)
+                nc.vector.tensor_tensor(big[:, pl], mag[:, pl, 0, :], mag[:, pl, 1, :], ALU.max)
+                nc.scalar.activation(root[:, pl], big[:, pl], ACT.Abs_reciprocal_sqrt, bias=shift[:])
+                nc.scalar.activation(inv[:, pl], root[:, pl], ACT.Square)
+            prod = keep.tile([P, PACK, n], F32, name=f"prod{c}")
+            for t in range(PACK):
+                nc.vector.scalar_tensor_tensor(
+                    prod[:, t], ab[:, t, 0, :], gs_sb[:, t : t + 1], ab[:, t, 1, :], ALU.mult, ALU.mult
+                )
+            st[c] = (prod, inv)
+
+        def finish(c):
+            n, j0 = CHUNKS[c], starts[c]
+            prod, inv = st[c]
+            z = keep.tile([P, n, PACK], BF16, name=f"z{c}", align_bytes=64)
+            walk = "p t (g i) -> p g t i"
+            nc.vector.tensor_tensor(
+                z[:].rearrange("p (g i) t -> p g t i", i=4),
+                prod[:].rearrange(walk, i=4), inv[:].rearrange(walk, i=4), ALU.mult,
+            )
+            z_codes = keep.tile([P, n], U32, name=f"z_codes{c}", align_bytes=64)
+            z_plane = keep.tile([P, n], U8, name=f"z_plane{c}", align_bytes=64)
+            nc.vector.quantize_mx(
+                out=z_codes[:].bitcast(FP8X4), scales=z_plane[:], in_=z[:].rearrange("p n t -> p (n t)")
+            )
+            per_bank = 512 // n
+            for b0 in range(0, PACK, per_bank):
+                o_ps = psum.tile([P, per_bank, n], F32, name=f"o_ps{c}_{b0}")
+                for b in range(per_bank):
+                    cols = slice(P * (b0 + b), P * (b0 + b + 1))
+                    nc.tensor.matmul_mx(
+                        out=o_ps[:, b, :], lhsT=d_codes[:, cols].bitcast(FP8X4), lhsT_scale=d_plane[:, cols],
+                        rhs=z_codes[:].bitcast(FP8X4), rhs_scale=z_plane[:], start=True, stop=True,
+                    )
+                o_sb = keep.tile([P, per_bank, n], F32, name=f"o_sb{c}_{b0}")
+                nc.scalar.activation(o_sb[:], o_ps[:], ACT.Copy, scale=0.0625)
+                dst = out.rearrange("(b p) j -> p b j", p=P)[:, b0 : b0 + per_bank, j0 : j0 + n]
+                nc.sync.dma_start(dst, o_sb[:])
+
+        gather(0)
+        larger(0)
+        gather(1)
+        nc.vector.tensor_copy(d_codes[:], dw_table[:].indirect(kq_sb[:]))
+        finish(0)
+        larger(1)
+        gather(2)
+        larger(2)
+        finish(1)
+        finish(2)

@@ -17,8 +17,8 @@ ACT = mybir.ActivationFunctionType
 
 P = 128
 PACK = 4
-CHUNKS = (256, 128, 128)
-M_VEC = 40
+CHUNKS = ((0, 256), (256, 128), (384, 128))
+M_VEC = 42
 
 
 def tile_picked_minsum2_none_p_kernel(
@@ -29,24 +29,30 @@ def tile_picked_minsum2_none_p_kernel(
         keep = ctx.enter_context(tc.tile_pool(name="keep", bufs=1))
         psum = ctx.enter_context(tc.psum_pool(name="psum", bufs=1))
 
+        def sb(shape, dtype, name, tag=None):
+            return keep.tile(shape, dtype, name=name, tag=tag or name, align_bytes=64)
+
         def load_list(name, src):
             t = keep.tile([P, S // 16], U16, name=name)
             nc.sync.dma_start(t[:], src)
             return t
 
-        xs_table = keep.tile([P, T], U8, name="xs_table")
-        ds_table = keep.tile([P, G], U8, name="ds_table")
-        d_plane = keep.tile([P, H], U8, name="d_plane", align_bytes=64)
-        seed = keep.tile([P, 1], F32, name="seed")
-        shift = keep.tile([P, 1], F32, name="shift")
+        xs_table = sb([P, T], U8, "xs_table")
+        ds_table = sb([P, G], U8, "ds_table")
+        d_plane = sb([P, H], U8, "d_plane")
+        seed = sb([P, 1], F32, "seed")
+        shift = sb([P, 1], F32, "shift")
         nc.vector.memset(xs_table[:].bitcast(I32), 0)
         nc.vector.memset(seed[:], 400.0)
         nc.scalar.activation(shift[:], seed[:], ACT.Abs_reciprocal_sqrt)
         nc.vector.memset(ds_table[:].bitcast(I32), 0)
         nc.vector.memset(d_plane[:].bitcast(I32), 0)
+        y = [sb([P, 2 * S], F32, f"y{t}") for t in range(PACK - 1)] + [sb([P, S], F32, "y3")]
+        for t in range(PACK - 1):
+            nc.gpsimd.memset(y[t][:, S:], 0.0)
 
         offs_sb = load_list("offs_sb", offs)
-        xw_table = keep.tile([P, T], U32, name="xw_table")
+        xw_table = sb([P, T], U32, "xw_table")
         nc.sync.dma_start(xw_table[:].bitcast(I32), x_words[0].rearrange("p n t -> p (n t)").bitcast(I32))
         xs_rows = x_scales[0].bitcast(I32)
         for q in range(4):
@@ -54,125 +60,153 @@ def tile_picked_minsum2_none_p_kernel(
         w_rows = w1.rearrange("(p j) c -> p j c", j=PACK)
         w_raw = []
         for h in range(2):
-            t = keep.tile([P, PACK, H // 2], F32, name=f"w_raw{h}")
-            nc.sync.dma_start(t[:], w_rows[:, :, h * (H // 2) : (h + 1) * (H // 2)])
-            w_raw.append(t)
+            piece = sb([P, PACK, H // 2], F32, f"w_raw{h}")
+            nc.sync.dma_start(piece[:], w_rows[:, :, h * (H // 2) : (h + 1) * (H // 2)])
+            w_raw.append(piece)
         kq_sb = load_list("kq_sb", kq)
         ds_rows = d_scales[0].bitcast(I32)
         for e in range(2):
             nc.sync.dma_start(ds_table[:].bitcast(I32)[e:P:16, :], ds_rows[e:16:2, :])
         c1_sb = load_list("c1_sb", c1)
         c2_sb = load_list("c2_sb", c2)
-        gs_sb = keep.tile([P, PACK], F32, name="gs_sb")
+        gs_sb = sb([P, PACK], F32, "gs_sb")
         nc.sync.dma_start(gs_sb[:], gs.rearrange("(p t) o -> p (t o)", t=PACK))
-        dw_table = keep.tile([P, G], U32, name="dw_table")
+        dw_table = sb([P, G], U32, "dw_table")
         nc.sync.dma_start(dw_table[:].bitcast(I32), d_words[0].rearrange("p n t -> p (n t)").bitcast(I32))
 
-        x_codes = keep.tile([P, S], U32, name="x_codes", align_bytes=64)
-        x_plane = keep.tile([P, S], U8, name="x_plane", align_bytes=64)
+        x_codes = sb([P, S], U32, "x_codes")
+        x_plane = sb([P, S], U8, "x_plane")
         nc.vector.tensor_copy(x_codes[:], xw_table[:].indirect(offs_sb[:]))
         nc.vector.tensor_copy(x_plane[:], xs_table[:].indirect(offs_sb[:]))
 
-        w_bf = keep.tile([P, PACK, P, PACK], BF16, name="w_bf", align_bytes=64)
-
-        def deal(copy, h, m0, m1):
+        w_bf = sb([P, PACK, P, PACK], BF16, "w_bf")
+        for copy, h, m0, m1 in (
+            (nc.scalar.copy, 0, 0, 64), (nc.vector.tensor_copy, 1, 0, M_VEC), (nc.scalar.copy, 1, M_VEC, 64)
+        ):
             src = w_raw[h][:, :, PACK * m0 : PACK * m1].rearrange("p j (m t) -> p m j t", t=PACK)
-            dst = w_bf[:, :, 64 * h + m0 : 64 * h + m1, :].rearrange("p t m j -> p m j t")
-            copy(dst, src)
-
-        deal(nc.scalar.copy, 0, 0, 64)
-        deal(nc.vector.tensor_copy, 1, 0, M_VEC)
-        deal(nc.scalar.copy, 1, M_VEC, 64)
-
-        y = []
-        for t in range(PACK):
-            w_codes = keep.tile([P, P], U32, name=f"w_codes{t}", align_bytes=64)
-            w_plane = keep.tile([P, P], U8, name=f"w_plane{t}", align_bytes=64)
+            copy(w_bf[:, :, 64 * h + m0 : 64 * h + m1, :].rearrange("p t m j -> p m j t"), src)
+        w_codes = sb([P, H], U32, "w_codes")
+        w_plane = sb([P, H], U8, "w_plane")
+        for t0, t1 in ((0, 1), (1, 2), (2, 4)):
             nc.vector.quantize_mx(
-                out=w_codes[:].bitcast(FP8X4), scales=w_plane[:], in_=w_bf[:, t].rearrange("p m j -> p (m j)")
+                out=w_codes[:, P * t0 : P * t1].bitcast(FP8X4),
+                scales=w_plane[:, P * t0 : P * t1],
+                in_=w_bf[:, t0:t1].rearrange("p t m j -> p (t m j)"),
             )
-            y_ps = psum.tile([P, S], F32, name=f"y_ps{t}")
+        half = S // 2
+
+        def project(t, j0, n, bank):
+            rows, cols = slice(P * t, P * (t + 1)), slice(j0, j0 + n)
+            y_ps = psum.tile([P, n], F32, name=f"y_ps{t}_{j0}", tag=bank)
             nc.tensor.matmul_mx(
-                out=y_ps[:], lhsT=w_codes[:].bitcast(FP8X4), lhsT_scale=w_plane[:],
-                rhs=x_codes[:].bitcast(FP8X4), rhs_scale=x_plane[:], start=True, stop=True,
+                out=y_ps[:], lhsT=w_codes[:, rows].bitcast(FP8X4), lhsT_scale=w_plane[:, rows],
+                rhs=x_codes[:, cols].bitcast(FP8X4), rhs_scale=x_plane[:, cols], start=True, stop=True,
             )
-            y_t = keep.tile([P, S], F32, name=f"y{t}")
-            nc.scalar.copy(y_t[:], y_ps[:])
-            y.append(y_t)
+            nc.scalar.copy(y[t][:, cols], y_ps[:])
 
-        ds_picked = keep.tile([P, H], U8, name="ds_picked")
-        nc.vector.tensor_copy(ds_picked[:], ds_table[:].indirect(kq_sb[:]))
-        for i in range(4):
-            first = 16 * (i // 2) + i % 2
-            nc.sync.dma_start(d_plane[:].bitcast(I32)[i:P:32, :], ds_picked[:].bitcast(I32)[first:P:32, :])
-        d_codes = keep.tile([P, H], U32, name="d_codes", align_bytes=64)
+        project(0, 0, half, "bank0")
+        project(0, half, half, "bank1")
+        for t in range(1, PACK):
+            project(t, 0, S, f"bank{t + 1}")
 
-        starts = [sum(CHUNKS[:c]) for c in range(len(CHUNKS))]
-        st = {}
+        def pick_d_scales(h, after):
+            cols = slice(h * half // 4, (h + 1) * half // 4)
+            picked = sb([P, half], U8, f"ds_picked{h}", tag=after)
+            nc.vector.tensor_copy(picked[:], ds_table[:].indirect(kq_sb[:, h * half // 16 : (h + 1) * half // 16]))
+            for i in range(4):
+                first = 16 * (i // 2) + i % 2
+                nc.sync.dma_start(d_plane[:].bitcast(I32)[i:P:32, cols], picked[:].bitcast(I32)[first:P:32, :])
 
-        def gather(c):
-            n, j0 = CHUNKS[c], starts[c]
-            ab = keep.tile([P, PACK, 2, n], F32, name=f"ab{c}")
-            mag = keep.tile([P, PACK, 2, n], F32, name=f"mag{c}")
-            for t in range(PACK):
-                for s, lst in enumerate((c1_sb, c2_sb)):
-                    nc.vector.tensor_copy(ab[:, t, s, :], y[t][:].indirect(lst[:, j0 // 16 : (j0 + n) // 16]))
-                nc.scalar.activation(mag[:, t], ab[:, t], ACT.Abs)
-            st[c] = (ab, mag)
+        pick_d_scales(0, "w_bf")
+        d_codes = sb([P, H], U32, "d_codes")
 
-        def larger(c):
-            n = CHUNKS[c]
-            ab, mag = st[c]
-            big = keep.tile([P, PACK, n], F32, name=f"big{c}")
-            root = keep.tile([P, PACK, n], F32, name=f"root{c}")
-            inv = keep.tile([P, PACK, n], F32, name=f"inv{c}")
-            for u in range(2):
-                pl = slice(2 * u, 2 * u + 2)
-                nc.vector.tensor_tensor(big[:, pl], mag[:, pl, 0, :], mag[:, pl, 1, :], ALU.max)
-                nc.scalar.activation(root[:, pl], big[:, pl], ACT.Abs_reciprocal_sqrt, bias=shift[:])
-                nc.scalar.activation(inv[:, pl], root[:, pl], ACT.Square)
-            prod = keep.tile([P, PACK, n], F32, name=f"prod{c}")
-            for t in range(PACK):
-                nc.vector.scalar_tensor_tensor(
-                    prod[:, t], ab[:, t, 0, :], gs_sb[:, t : t + 1], ab[:, t, 1, :], ALU.mult, ALU.mult
-                )
-            st[c] = (prod, inv)
+        prod = sb([P, PACK, S], F32, "prod")
+        inv = sb([P, PACK, S], F32, "inv")
+        pairs, mags = {}, {}
 
-        def finish(c):
-            n, j0 = CHUNKS[c], starts[c]
-            prod, inv = st[c]
-            z = keep.tile([P, n, PACK], BF16, name=f"z{c}", align_bytes=64)
+        def fetch(t, j0, n, after=None):
+            ab = sb([P, 2, n], F32, f"ab{t}_{j0}", tag=after)
+            mag = sb([P, 2, n], F32, f"mag{t}_{j0}")
+            for s, lst in enumerate((c1_sb, c2_sb)):
+                nc.vector.tensor_copy(ab[:, s, :], y[t][:].indirect(lst[:, j0 // 16 : (j0 + n) // 16]))
+            nc.scalar.activation(mag[:], ab[:], ACT.Abs)
+            pairs[t, j0], mags[t, j0] = ab, mag
+
+        def invert(t, j0, n):
+            mag = mags[t, j0]
+            big = sb([P, n], F32, f"big{t}_{j0}")
+            root = sb([P, n], F32, f"root{t}_{j0}")
+            nc.vector.tensor_tensor(big[:], mag[:, 0, :], mag[:, 1, :], ALU.max)
+            nc.scalar.activation(root[:], big[:], ACT.Abs_reciprocal_sqrt, bias=shift[:])
+            nc.scalar.activation(inv[:, t, j0 : j0 + n], root[:], ACT.Square)
+
+        def multiply(t, j0, n):
+            ab = pairs[t, j0]
+            nc.vector.scalar_tensor_tensor(
+                prod[:, t, j0 : j0 + n], ab[:, 0, :], gs_sb[:, t : t + 1], ab[:, 1, :], ALU.mult, ALU.mult
+            )
+
+        zs = {}
+
+        def weave(j0, n):
+            z = sb([P, n, PACK], BF16, f"z{j0}")
             walk = "p t (g i) -> p g t i"
             nc.vector.tensor_tensor(
                 z[:].rearrange("p (g i) t -> p g t i", i=4),
-                prod[:].rearrange(walk, i=4), inv[:].rearrange(walk, i=4), ALU.mult,
+                prod[:, :, j0 : j0 + n].rearrange(walk, i=4),
+                inv[:, :, j0 : j0 + n].rearrange(walk, i=4),
+                ALU.mult,
             )
-            z_codes = keep.tile([P, n], U32, name=f"z_codes{c}", align_bytes=64)
-            z_plane = keep.tile([P, n], U8, name=f"z_plane{c}", align_bytes=64)
+            zs[j0] = z
+
+        def finish(j0, n, banks, split):
+            z_codes = sb([P, n], U32, f"z_codes{j0}")
+            z_plane = sb([P, n], U8, f"z_plane{j0}")
             nc.vector.quantize_mx(
-                out=z_codes[:].bitcast(FP8X4), scales=z_plane[:], in_=z[:].rearrange("p n t -> p (n t)")
+                out=z_codes[:].bitcast(FP8X4), scales=z_plane[:], in_=zs[j0][:].rearrange("p n t -> p (n t)")
             )
-            per_bank = 512 // n
-            for b0 in range(0, PACK, per_bank):
-                o_ps = psum.tile([P, per_bank, n], F32, name=f"o_ps{c}_{b0}")
+            per_bank = PACK // len(banks)
+            for u, bank in enumerate(banks):
+                b0 = u * per_bank
+                o_ps = psum.tile([P, per_bank, n], F32, name=f"o_ps{j0}_{u}", tag=bank)
                 for b in range(per_bank):
                     cols = slice(P * (b0 + b), P * (b0 + b + 1))
                     nc.tensor.matmul_mx(
                         out=o_ps[:, b, :], lhsT=d_codes[:, cols].bitcast(FP8X4), lhsT_scale=d_plane[:, cols],
                         rhs=z_codes[:].bitcast(FP8X4), rhs_scale=z_plane[:], start=True, stop=True,
                     )
-                o_sb = keep.tile([P, per_bank, n], F32, name=f"o_sb{c}_{b0}")
-                nc.scalar.activation(o_sb[:], o_ps[:], ACT.Copy, scale=0.0625)
+                o_sb = sb([P, per_bank, n], F32, f"o_sb{j0}_{u}")
                 dst = out.rearrange("(b p) j -> p b j", p=P)[:, b0 : b0 + per_bank, j0 : j0 + n]
+                if split and u == 1:
+                    nc.vector.tensor_scalar(o_sb[:], o_ps[:], 0.0625, None, ALU.mult)
+                else:
+                    nc.scalar.activation(o_sb[:], o_ps[:], ACT.Copy, scale=0.0625)
                 nc.sync.dma_start(dst, o_sb[:])
 
-        gather(0)
-        larger(0)
-        gather(1)
+        last = PACK - 1
+        fetch(0, 0, S)
+        fetch(1, 0, S)
+        multiply(0, 0, S)
+        pick_d_scales(1, "ab0_0")
+        invert(0, 0, S)
+        fetch(2, 0, S, after="mag0_0")
+        invert(1, 0, S)
+        multiply(1, 0, S)
         nc.vector.tensor_copy(d_codes[:], dw_table[:].indirect(kq_sb[:]))
-        finish(0)
-        larger(1)
-        gather(2)
-        larger(2)
-        finish(1)
-        finish(2)
+        fetch(last, *CHUNKS[0], after="mag1_0")
+        invert(2, 0, S)
+        multiply(2, 0, S)
+        fetch(last, *CHUNKS[1], after="mag2_0")
+        invert(last, *CHUNKS[0])
+        multiply(last, *CHUNKS[0])
+        fetch(last, *CHUNKS[2], after="mag3_0")
+        invert(last, *CHUNKS[1])
+        multiply(last, *CHUNKS[1])
+        weave(*CHUNKS[0])
+        invert(last, *CHUNKS[2])
+        finish(*CHUNKS[0], ("bank5", "bank6"), False)
+        weave(*CHUNKS[1])
+        multiply(last, *CHUNKS[2])
+        finish(*CHUNKS[1], ("bank7",), False)
+        weave(*CHUNKS[2])
+        finish(*CHUNKS[2], ("bank0", "bank1"), True)

@@ -51,9 +51,9 @@ def tile_picked_minsum2_none_p_kernel(
         for t in range(PACK - 1):
             nc.gpsimd.memset(y[t][:, S:], 0.0)
 
-        offs_sb = load_list("offs_sb", offs)
         xw_table = sb([P, T], U32, "xw_table")
         nc.sync.dma_start(xw_table[:].bitcast(I32), x_words[0].rearrange("p n t -> p (n t)").bitcast(I32))
+        offs_sb = load_list("offs_sb", offs)
         xs_rows = x_scales[0].bitcast(I32)
         for q in range(4):
             nc.sync.dma_start(xs_table[:].bitcast(I32)[32 * q : 32 * q + 4, :], xs_rows[4 * q : 4 * q + 4, :])
@@ -109,34 +109,45 @@ def tile_picked_minsum2_none_p_kernel(
         for t in range(1, PACK):
             project(t, 0, S, f"bank{t + 1}")
 
-        def pick_d_scales(h, after):
-            cols = slice(h * half // 4, (h + 1) * half // 4)
-            picked = sb([P, half], U8, f"ds_picked{h}", tag=after)
-            nc.vector.tensor_copy(picked[:], ds_table[:].indirect(kq_sb[:, h * half // 16 : (h + 1) * half // 16]))
-            for i in range(4):
-                first = 16 * (i // 2) + i % 2
-                nc.sync.dma_start(d_plane[:].bitcast(I32)[i:P:32, cols], picked[:].bitcast(I32)[first:P:32, :])
-
-        pick_d_scales(0, "w_bf")
-        d_codes = sb([P, H], U32, "d_codes")
+        ds_picked = sb([P, H], U8, "ds_picked", tag="w_bf")
+        nc.vector.tensor_copy(ds_picked[:], ds_table[:].indirect(kq_sb[:]))
+        for i in range(4):
+            first = 16 * (i // 2) + i % 2
+            nc.sync.dma_start(d_plane[:].bitcast(I32)[i:P:32, :], ds_picked[:].bitcast(I32)[first:P:32, :])
 
         prod = sb([P, PACK, S], F32, "prod")
         inv = sb([P, PACK, S], F32, "inv")
         pairs, mags = {}, {}
 
+        def fetch_whole(t, after=None):
+            a = sb([P, S], F32, f"a{t}", tag=after)
+            b = sb([P, S], F32, f"b{t}")
+            mag_a = [sb([P, half], F32, f"mag_a{t}_{h}") for h in range(2)]
+            mag_b = sb([P, S], F32, f"mag_b{t}")
+            ga = sb([P, S], F32, f"ga{t}")
+            nc.vector.tensor_copy(a[:], y[t][:].indirect(c1_sb[:]))
+            for h in range(2):
+                nc.scalar.activation(mag_a[h][:], a[:, h * half : (h + 1) * half], ACT.Abs)
+            nc.gpsimd.tensor_scalar(ga[:], a[:], gs_sb[:, t : t + 1], 0.0, ALU.mult, ALU.add)
+            nc.vector.tensor_copy(b[:], y[t][:].indirect(c2_sb[:]))
+            nc.scalar.activation(mag_b[:], b[:], ACT.Abs)
+            nc.gpsimd.tensor_tensor(prod[:, t, :], ga[:], b[:], ALU.mult)
+            mags[t, 0] = [(h * half, mag_a[h][:], mag_b[:, h * half : (h + 1) * half]) for h in range(2)]
+
         def fetch(t, j0, n, after=None):
+            cols = slice(j0 // 16, (j0 + n) // 16)
             ab = sb([P, 2, n], F32, f"ab{t}_{j0}", tag=after)
             mag = sb([P, 2, n], F32, f"mag{t}_{j0}")
             for s, lst in enumerate((c1_sb, c2_sb)):
-                nc.vector.tensor_copy(ab[:, s, :], y[t][:].indirect(lst[:, j0 // 16 : (j0 + n) // 16]))
+                nc.vector.tensor_copy(ab[:, s, :], y[t][:].indirect(lst[:, cols]))
             nc.scalar.activation(mag[:], ab[:], ACT.Abs)
-            pairs[t, j0], mags[t, j0] = ab, mag
+            pairs[t, j0], mags[t, j0] = ab, [(0, mag[:, 0, :], mag[:, 1, :])]
 
         def invert(t, j0, n):
-            mag = mags[t, j0]
             big = sb([P, n], F32, f"big{t}_{j0}")
             root = sb([P, n], F32, f"root{t}_{j0}")
-            nc.vector.tensor_tensor(big[:], mag[:, 0, :], mag[:, 1, :], ALU.max)
+            for c0, mag_a, mag_b in mags[t, j0]:
+                nc.vector.tensor_tensor(big[:, c0 : c0 + mag_a.shape[1]], mag_a, mag_b, ALU.max)
             nc.scalar.activation(root[:], big[:], ACT.Abs_reciprocal_sqrt, bias=shift[:])
             nc.scalar.activation(inv[:, t, j0 : j0 + n], root[:], ACT.Square)
 
@@ -184,29 +195,23 @@ def tile_picked_minsum2_none_p_kernel(
                 nc.sync.dma_start(dst, o_sb[:])
 
         last = PACK - 1
-        fetch(0, 0, S)
-        fetch(1, 0, S)
-        multiply(0, 0, S)
-        pick_d_scales(1, "ab0_0")
-        invert(0, 0, S)
-        fetch(2, 0, S, after="mag0_0")
-        invert(1, 0, S)
-        multiply(1, 0, S)
+        fetch_whole(0)
+        fetch_whole(1)
+        d_codes = sb([P, H], U32, "d_codes")
         nc.vector.tensor_copy(d_codes[:], dw_table[:].indirect(kq_sb[:]))
-        fetch(last, *CHUNKS[0], after="mag1_0")
+        invert(0, 0, S)
+        fetch_whole(2, after="mag_a0_0")
+        invert(1, 0, S)
+        fetch(last, 0, half, after="mag_a1_0")
         invert(2, 0, S)
-        multiply(2, 0, S)
-        fetch(last, *CHUNKS[1], after="mag2_0")
-        invert(last, *CHUNKS[0])
-        multiply(last, *CHUNKS[0])
-        fetch(last, *CHUNKS[2], after="mag3_0")
-        invert(last, *CHUNKS[1])
-        multiply(last, *CHUNKS[1])
+        fetch(last, half, half, after="mag_a2_0")
+        invert(last, 0, half)
+        multiply(last, 0, half)
+        invert(last, half, half)
         weave(*CHUNKS[0])
-        invert(last, *CHUNKS[2])
+        multiply(last, half, half)
         finish(*CHUNKS[0], ("bank5", "bank6"), False)
         weave(*CHUNKS[1])
-        multiply(last, *CHUNKS[2])
         finish(*CHUNKS[1], ("bank7",), False)
         weave(*CHUNKS[2])
         finish(*CHUNKS[2], ("bank0", "bank1"), True)

@@ -115,33 +115,40 @@ def tile_picked_minsum2_none_p_kernel(
             first = 16 * (i // 2) + i % 2
             nc.sync.dma_start(d_plane[:].bitcast(I32)[i:P:32, :], ds_picked[:].bitcast(I32)[first:P:32, :])
 
-        prod = sb([P, PACK, S], F32, "prod")
-        inv = sb([P, PACK, S], F32, "inv")
-        pairs, mags = {}, {}
+        prod = sb([P, 2, PACK, half], F32, "prod")
+        inv = sb([P, 2, PACK, half], F32, "inv")
+        pairs, mags, scaled = {}, {}, {}
+
+        def plane(tile, t, j0, n):
+            if n < S:
+                return tile[:, j0 // half, t, j0 % half : j0 % half + n]
+            return tile[:, :, t, :]
+
+        def halves(ap):
+            return ap.rearrange("p (h j) -> p h j", j=half)
 
         def fetch_whole(t, after=None):
             a = sb([P, S], F32, f"a{t}", tag=after)
             b = sb([P, S], F32, f"b{t}")
             mag_a = [sb([P, half], F32, f"mag_a{t}_{h}") for h in range(2)]
-            mag_b = sb([P, S], F32, f"mag_b{t}")
+            mag_b = plane(prod, t + 1, 0, S)
             ga = sb([P, S], F32, f"ga{t}")
             nc.vector.tensor_copy(a[:], y[t][:].indirect(c1_sb[:]))
             for h in range(2):
                 nc.scalar.activation(mag_a[h][:], a[:, h * half : (h + 1) * half], ACT.Abs)
             nc.gpsimd.tensor_scalar(ga[:], a[:], gs_sb[:, t : t + 1], 0.0, ALU.mult, ALU.add)
             nc.vector.tensor_copy(b[:], y[t][:].indirect(c2_sb[:]))
-            nc.scalar.activation(mag_b[:], b[:], ACT.Abs)
-            nc.gpsimd.tensor_tensor(prod[:, t, :], ga[:], b[:], ALU.mult)
-            mags[t, 0] = [(h * half, mag_a[h][:], mag_b[:, h * half : (h + 1) * half]) for h in range(2)]
+            nc.scalar.activation(mag_b, halves(b[:]), ACT.Abs)
+            scaled[t] = (ga, b)
+            mags[t, 0] = [(h * half, mag_a[h][:], mag_b[:, h, :]) for h in range(2)]
 
         def fetch(t, j0, n, after=None):
             cols = slice(j0 // 16, (j0 + n) // 16)
             ab = sb([P, 2, n], F32, f"ab{t}_{j0}", tag=after)
-            mag = sb([P, 2, n], F32, f"mag{t}_{j0}")
             for s, lst in enumerate((c1_sb, c2_sb)):
                 nc.vector.tensor_copy(ab[:, s, :], y[t][:].indirect(lst[:, cols]))
-            nc.scalar.activation(mag[:], ab[:], ACT.Abs)
-            pairs[t, j0], mags[t, j0] = ab, [(0, mag[:, 0, :], mag[:, 1, :])]
+            pairs[t, j0] = ab
+            return ab
 
         def invert(t, j0, n):
             big = sb([P, n], F32, f"big{t}_{j0}")
@@ -149,13 +156,17 @@ def tile_picked_minsum2_none_p_kernel(
             for c0, mag_a, mag_b in mags[t, j0]:
                 nc.vector.tensor_tensor(big[:, c0 : c0 + mag_a.shape[1]], mag_a, mag_b, ALU.max)
             nc.scalar.activation(root[:], big[:], ACT.Abs_reciprocal_sqrt, bias=shift[:])
-            nc.scalar.activation(inv[:, t, j0 : j0 + n], root[:], ACT.Square)
+            nc.scalar.activation(plane(inv, t, j0, n), halves(root[:]) if n == S else root[:], ACT.Square)
 
         def multiply(t, j0, n):
             ab = pairs[t, j0]
             nc.vector.scalar_tensor_tensor(
-                prod[:, t, j0 : j0 + n], ab[:, 0, :], gs_sb[:, t : t + 1], ab[:, 1, :], ALU.mult, ALU.mult
+                prod[:, j0 // half, t, :], ab[:, 0, :], gs_sb[:, t : t + 1], ab[:, 1, :], ALU.mult, ALU.mult
             )
+
+        def multiply_whole(t):
+            ga, b = scaled[t]
+            nc.gpsimd.tensor_tensor(plane(prod, t, 0, S), halves(ga[:]), halves(b[:]), ALU.mult)
 
         zs = {}
 
@@ -163,9 +174,9 @@ def tile_picked_minsum2_none_p_kernel(
             z = sb([P, n, PACK], BF16, f"z{j0}")
             walk = "p t (g i) -> p g t i"
             nc.vector.tensor_tensor(
-                z[:].rearrange("p (g i) t -> p g t i", i=4),
-                prod[:, :, j0 : j0 + n].rearrange(walk, i=4),
-                inv[:, :, j0 : j0 + n].rearrange(walk, i=4),
+                z[:].rearrange("p (g i) t -> p g t i", i=2),
+                prod[:, j0 // half, :, j0 % half : j0 % half + n].rearrange(walk, i=2),
+                inv[:, j0 // half, :, j0 % half : j0 % half + n].rearrange(walk, i=2),
                 ALU.mult,
             )
             zs[j0] = z
@@ -188,29 +199,45 @@ def tile_picked_minsum2_none_p_kernel(
                     )
                 o_sb = sb([P, per_bank, n], F32, f"o_sb{j0}_{u}")
                 dst = out.rearrange("(b p) j -> p b j", p=P)[:, b0 : b0 + per_bank, j0 : j0 + n]
-                if split and u == 1:
+                if split:
                     nc.vector.tensor_scalar(o_sb[:], o_ps[:], 0.0625, None, ALU.mult)
                 else:
                     nc.scalar.activation(o_sb[:], o_ps[:], ACT.Copy, scale=0.0625)
-                nc.sync.dma_start(dst, o_sb[:])
+                (nc.scalar if split and u == 1 else nc.sync).dma_start(dst, o_sb[:])
 
         last = PACK - 1
         fetch_whole(0)
+        multiply_whole(0)
         fetch_whole(1)
-        d_codes = sb([P, H], U32, "d_codes")
-        nc.vector.tensor_copy(d_codes[:], dw_table[:].indirect(kq_sb[:]))
         invert(0, 0, S)
+        multiply_whole(1)
         fetch_whole(2, after="mag_a0_0")
         invert(1, 0, S)
-        fetch(last, 0, half, after="mag_a1_0")
-        invert(2, 0, S)
-        fetch(last, half, half, after="mag_a2_0")
+        multiply_whole(2)
+        ab = fetch(last, 0, half, after="mag_a1_0")
+        mag = sb([P, 2, half], F32, "mag3_0")
+        nc.scalar.activation(mag[:], ab[:], ACT.Abs)
+        mags[last, 0] = [(0, mag[:, 0, :], mag[:, 1, :])]
+        d_codes = sb([P, H], U32, "d_codes", tag="mag_a1_1")
+        nc.vector.tensor_copy(d_codes[:], dw_table[:].indirect(kq_sb[:]))
+        lo, hi = mags[2, 0]
+        mags[2, 0], mags[2, half] = [lo], [(0, hi[1], hi[2])]
+        invert(2, 0, half)
         invert(last, 0, half)
+        invert(2, half, half)
         multiply(last, 0, half)
-        invert(last, half, half)
+        ab = fetch(last, half, half, after="mag3_0")
+        mag_a = sb([P, half], F32, "mag_a3", tag="root3_0")
+        mag_b = plane(prod, last, half, half)
+        nc.scalar.activation(mag_a[:], ab[:, 0, :], ACT.Abs)
+        nc.scalar.activation(mag_b, ab[:, 1, :], ACT.Abs)
         weave(*CHUNKS[0])
-        multiply(last, half, half)
+        for j0, n in CHUNKS[1:]:
+            cols = slice(j0 - half, j0 - half + n)
+            mags[last, j0] = [(0, mag_a[:, cols], mag_b[:, cols])]
+            invert(last, j0, n)
         finish(*CHUNKS[0], ("bank5", "bank6"), False)
+        multiply(last, half, half)
         weave(*CHUNKS[1])
         finish(*CHUNKS[1], ("bank7",), False)
         weave(*CHUNKS[2])

from contextlib import ExitStack

import concourse.mybir as mybir

K, T, S, H, G = 512, 2048, 512, 512, 2048
FLOPS = 2 * K * H * S * 2

F32 = mybir.dt.float32
BF16 = mybir.dt.bfloat16
I32 = mybir.dt.int32
U32 = mybir.dt.uint32
U16 = mybir.dt.uint16
U8 = mybir.dt.uint8
FP8X4 = mybir.dt.float8_e4m3fn_x4
ALU = mybir.AluOpType
ACT = mybir.ActivationFunctionType

P = 128
PACK = 4
CHUNKS = ((0, 256), (256, 128), (384, 128))
M_VEC = 42


def tile_picked_minsum2_none_p_kernel(
    tc, x_words, x_scales, w1, gs, d_words, d_scales, offs, c1, c2, kq, out
):
    nc = tc.nc
    with ExitStack() as ctx:
        keep = ctx.enter_context(tc.tile_pool(name="keep", bufs=1))
        psum = ctx.enter_context(tc.psum_pool(name="psum", bufs=1))

        def sb(shape, dtype, name, tag=None):
            return keep.tile(shape, dtype, name=name, tag=tag or name, align_bytes=64)

        def load_list(name, src):
            t = keep.tile([P, S // 16], U16, name=name)
            nc.sync.dma_start(t[:], src)
            return t

        xs_table = sb([P, T], U8, "xs_table")
        ds_table = sb([P, G], U8, "ds_table")
        d_plane = sb([P, H], U8, "d_plane")
        seed = sb([P, 1], F32, "seed")
        shift = sb([P, 1], F32, "shift")
        nc.vector.memset(xs_table[:].bitcast(I32), 0)
        nc.vector.memset(seed[:], 400.0)
        nc.scalar.activation(shift[:], seed[:], ACT.Abs_reciprocal_sqrt)
        nc.vector.memset(ds_table[:].bitcast(I32), 0)
        nc.vector.memset(d_plane[:].bitcast(I32), 0)
        y = [sb([P, 2 * S], F32, f"y{t}") for t in range(PACK - 1)] + [sb([P, S], F32, "y3")]
        for t in range(PACK - 1):
            nc.gpsimd.memset(y[t][:, S:], 0.0)

        xw_table = sb([P, T], U32, "xw_table")
        nc.sync.dma_start(xw_table[:].bitcast(I32), x_words[0].rearrange("p n t -> p (n t)").bitcast(I32))
        offs_sb = load_list("offs_sb", offs)
        xs_rows = x_scales[0].bitcast(I32)
        for q in range(4):
            nc.sync.dma_start(xs_table[:].bitcast(I32)[32 * q : 32 * q + 4, :], xs_rows[4 * q : 4 * q + 4, :])
        w_rows = w1.rearrange("(p j) c -> p j c", j=PACK)
        w_raw = []
        for h in range(2):
            piece = sb([P, PACK, H // 2], F32, f"w_raw{h}")
            nc.sync.dma_start(piece[:], w_rows[:, :, h * (H // 2) : (h + 1) * (H // 2)])
            w_raw.append(piece)
        kq_sb = load_list("kq_sb", kq)
        ds_rows = d_scales[0].bitcast(I32)
        for e in range(2):
            nc.sync.dma_start(ds_table[:].bitcast(I32)[e:P:16, :], ds_rows[e:16:2, :])
        c1_sb = load_list("c1_sb", c1)
        c2_sb = load_list("c2_sb", c2)
        gs_sb = sb([P, PACK], F32, "gs_sb")
        nc.sync.dma_start(gs_sb[:], gs.rearrange("(p t) o -> p (t o)", t=PACK))
        dw_table = sb([P, G], U32, "dw_table")
        nc.sync.dma_start(dw_table[:].bitcast(I32), d_words[0].rearrange("p n t -> p (n t)").bitcast(I32))

        x_codes = sb([P, S], U32, "x_codes")
        x_plane = sb([P, S], U8, "x_plane")
        nc.vector.tensor_copy(x_codes[:], xw_table[:].indirect(offs_sb[:]))
        nc.vector.tensor_copy(x_plane[:], xs_table[:].indirect(offs_sb[:]))

        w_bf = sb([P, PACK, P, PACK], BF16, "w_bf")
        for copy, h, m0, m1 in (
            (nc.scalar.copy, 0, 0, 64), (nc.vector.tensor_copy, 1, 0, M_VEC), (nc.scalar.copy, 1, M_VEC, 64)
        ):
            src = w_raw[h][:, :, PACK * m0 : PACK * m1].rearrange("p j (m t) -> p m j t", t=PACK)
            copy(w_bf[:, :, 64 * h + m0 : 64 * h + m1, :].rearrange("p t m j -> p m j t"), src)
        w_codes = sb([P, H], U32, "w_codes")
        w_plane = sb([P, H], U8, "w_plane")
        for t0, t1 in ((0, 1), (1, 2), (2, 4)):
            nc.vector.quantize_mx(
                out=w_codes[:, P * t0 : P * t1].bitcast(FP8X4),
                scales=w_plane[:, P * t0 : P * t1],
                in_=w_bf[:, t0:t1].rearrange("p t m j -> p (t m j)"),
            )
        half = S // 2

        def project(t, j0, n, bank):
            rows, cols = slice(P * t, P * (t + 1)), slice(j0, j0 + n)
            y_ps = psum.tile([P, n], F32, name=f"y_ps{t}_{j0}", tag=bank)
            nc.tensor.matmul_mx(
                out=y_ps[:], lhsT=w_codes[:, rows].bitcast(FP8X4), lhsT_scale=w_plane[:, rows],
                rhs=x_codes[:, cols].bitcast(FP8X4), rhs_scale=x_plane[:, cols], start=True, stop=True,
            )
            nc.scalar.copy(y[t][:, cols], y_ps[:])

        project(0, 0, half, "bank0")
        project(0, half, half, "bank1")
        for t in range(1, PACK):
            project(t, 0, S, f"bank{t + 1}")

        ds_picked = sb([P, H], U8, "ds_picked", tag="w_bf")
        nc.vector.tensor_copy(ds_picked[:], ds_table[:].indirect(kq_sb[:]))
        for i in range(4):
            first = 16 * (i // 2) + i % 2
            nc.sync.dma_start(d_plane[:].bitcast(I32)[i:P:32, :], ds_picked[:].bitcast(I32)[first:P:32, :])

        prod = sb([P, 2, PACK, half], F32, "prod")
        inv = sb([P, 2, PACK, half], F32, "inv")
        pairs, mags, scaled = {}, {}, {}

        def plane(tile, t, j0, n):
            if n < S:
                return tile[:, j0 // half, t, j0 % half : j0 % half + n]
            return tile[:, :, t, :]

        def halves(ap):
            return ap.rearrange("p (h j) -> p h j", j=half)

        def fetch_whole(t, after=None):
            a = sb([P, S], F32, f"a{t}", tag=after)
            b = sb([P, S], F32, f"b{t}")
            mag_a = [sb([P, half], F32, f"mag_a{t}_{h}") for h in range(2)]
            mag_b = plane(prod, t + 1, 0, S)
            ga = sb([P, S], F32, f"ga{t}")
            nc.vector.tensor_copy(a[:], y[t][:].indirect(c1_sb[:]))
            for h in range(2):
                nc.scalar.activation(mag_a[h][:], a[:, h * half : (h + 1) * half], ACT.Abs)
            nc.gpsimd.tensor_scalar(ga[:], a[:], gs_sb[:, t : t + 1], 0.0, ALU.mult, ALU.add)
            nc.vector.tensor_copy(b[:], y[t][:].indirect(c2_sb[:]))
            nc.scalar.activation(mag_b, halves(b[:]), ACT.Abs)
            scaled[t] = (ga, b)
            mags[t, 0] = [(h * half, mag_a[h][:], mag_b[:, h, :]) for h in range(2)]

        def fetch(t, j0, n, after=None):
            cols = slice(j0 // 16, (j0 + n) // 16)
            ab = sb([P, 2, n], F32, f"ab{t}_{j0}", tag=after)
            for s, lst in enumerate((c1_sb, c2_sb)):
                nc.vector.tensor_copy(ab[:, s, :], y[t][:].indirect(lst[:, cols]))
            pairs[t, j0] = ab
            return ab

        def invert(t, j0, n):
            big = sb([P, n], F32, f"big{t}_{j0}")
            root = sb([P, n], F32, f"root{t}_{j0}")
            for c0, mag_a, mag_b in mags[t, j0]:
                nc.vector.tensor_tensor(big[:, c0 : c0 + mag_a.shape[1]], mag_a, mag_b, ALU.max)
            nc.scalar.activation(root[:], big[:], ACT.Abs_reciprocal_sqrt, bias=shift[:])
            nc.scalar.activation(plane(inv, t, j0, n), halves(root[:]) if n == S else root[:], ACT.Square)

        def multiply(t, j0, n):
            ab = pairs[t, j0]
            nc.vector.scalar_tensor_tensor(
                prod[:, j0 // half, t, :], ab[:, 0, :], gs_sb[:, t : t + 1], ab[:, 1, :], ALU.mult, ALU.mult
            )

        def multiply_whole(t):
            ga, b = scaled[t]
            nc.gpsimd.tensor_tensor(plane(prod, t, 0, S), halves(ga[:]), halves(b[:]), ALU.mult)

        zs = {}

        def weave(j0, n):
            z = sb([P, n, PACK], BF16, f"z{j0}")
            walk = "p t (g i) -> p g t i"
            nc.vector.tensor_tensor(
                z[:].rearrange("p (g i) t -> p g t i", i=2),
                prod[:, j0 // half, :, j0 % half : j0 % half + n].rearrange(walk, i=2),
                inv[:, j0 // half, :, j0 % half : j0 % half + n].rearrange(walk, i=2),
                ALU.mult,
            )
            zs[j0] = z

        def finish(j0, n, banks, split):
            z_codes = sb([P, n], U32, f"z_codes{j0}")
            z_plane = sb([P, n], U8, f"z_plane{j0}")
            nc.vector.quantize_mx(
                out=z_codes[:].bitcast(FP8X4), scales=z_plane[:], in_=zs[j0][:].rearrange("p n t -> p (n t)")
            )
            per_bank = PACK // len(banks)
            for u, bank in enumerate(banks):
                b0 = u * per_bank
                o_ps = psum.tile([P, per_bank, n], F32, name=f"o_ps{j0}_{u}", tag=bank)
                for b in range(per_bank):
                    cols = slice(P * (b0 + b), P * (b0 + b + 1))
                    nc.tensor.matmul_mx(
                        out=o_ps[:, b, :], lhsT=d_codes[:, cols].bitcast(FP8X4), lhsT_scale=d_plane[:, cols],
                        rhs=z_codes[:].bitcast(FP8X4), rhs_scale=z_plane[:], start=True, stop=True,
                    )
                o_sb = sb([P, per_bank, n], F32, f"o_sb{j0}_{u}")
                dst = out.rearrange("(b p) j -> p b j", p=P)[:, b0 : b0 + per_bank, j0 : j0 + n]
                if split:
                    nc.vector.tensor_scalar(o_sb[:], o_ps[:], 0.0625, None, ALU.mult)
                else:
                    nc.scalar.activation(o_sb[:], o_ps[:], ACT.Copy, scale=0.0625)
                (nc.scalar if split and u == 1 else nc.sync).dma_start(dst, o_sb[:])

        last = PACK - 1
        fetch_whole(0)
        multiply_whole(0)
        fetch_whole(1)
        invert(0, 0, S)
        multiply_whole(1)
        fetch_whole(2, after="mag_a0_0")
        invert(1, 0, S)
        multiply_whole(2)
        ab = fetch(last, 0, half, after="mag_a1_0")
        mag = sb([P, 2, half], F32, "mag3_0")
        nc.scalar.activation(mag[:], ab[:], ACT.Abs)
        mags[last, 0] = [(0, mag[:, 0, :], mag[:, 1, :])]
        d_codes = sb([P, H], U32, "d_codes", tag="mag_a1_1")
        nc.vector.tensor_copy(d_codes[:], dw_table[:].indirect(kq_sb[:]))
        lo, hi = mags[2, 0]
        mags[2, 0], mags[2, half] = [lo], [(0, hi[1], hi[2])]
        invert(2, 0, half)
        invert(last, 0, half)
        invert(2, half, half)
        multiply(last, 0, half)
        ab = fetch(last, half, half, after="mag3_0")
        mag_a = sb([P, half], F32, "mag_a3", tag="root3_0")
        mag_b = plane(prod, last, half, half)
        nc.scalar.activation(mag_a[:], ab[:, 0, :], ACT.Abs)
        nc.scalar.activation(mag_b, ab[:, 1, :], ACT.Abs)
        weave(*CHUNKS[0])
        for j0, n in CHUNKS[1:]:
            cols = slice(j0 - half, j0 - half + n)
            mags[last, j0] = [(0, mag_a[:, cols], mag_b[:, cols])]
            invert(last, j0, n)
        finish(*CHUNKS[0], ("bank5", "bank6"), False)
        multiply(last, half, half)
        weave(*CHUNKS[1])
        finish(*CHUNKS[1], ("bank7",), False)
        weave(*CHUNKS[2])
        finish(*CHUNKS[2], ("bank0", "bank1"), True)
